import numpy as np
import ml_dtypes


def mxq(x, axis, fmt="e4m3"):
    dtype, down = {"e4m3": (ml_dtypes.float8_e4m3fn, 7), "e5m2": (ml_dtypes.float8_e5m2, 14)}[fmt]
    v = np.moveaxis(np.asarray(x, np.float32).astype(ml_dtypes.bfloat16).astype(np.float64), axis, -1)
    blocks = v.reshape(v.shape[:-1] + (-1, 32))
    amax = np.abs(blocks).max(-1, keepdims=True)
    byte = np.maximum(np.where(amax > 0, np.frexp(amax)[1] - 1 + 127, 0) - down, 1)
    scale = np.exp2(byte - 127.0)
    codes = (blocks / scale).astype(np.float32).astype(dtype).astype(np.float64)
    return np.moveaxis((codes * scale).reshape(v.shape), -1, axis)


WIDE = False


def mx_kscale(k):
    if not WIDE:
        return np.ones(k)
    levels = np.array([10, -10, 5, -5, 0])
    if k % 512:
        return np.exp2(np.random.permutation(np.resize(levels, k // 32))).repeat(32)
    a = np.empty((k // 512, 16))
    for p in range(k // 512):
        a[p, :8] = np.random.permutation(np.resize(levels, 8))
        for g in range(8):
            far = levels[np.abs(levels - a[p, g]) >= 10]
            a[p, g + 8] = far[np.random.randint(len(far))]
    return np.exp2(a.ravel()).repeat(32)


def f64(x):
    return np.asarray(x).astype(np.float64)


def striped(idx):
    return np.tile(idx.reshape(-1, 16).T, (8, 1)).astype(np.uint16)


def unstriped(offs):
    return offs[:16].T.reshape(-1).astype(np.int64)


E2M1 = np.array([0.0, 0.5, 1.0, 1.5, 2.0, 3.0, 4.0, 6.0, -0.0, -0.5, -1.0, -1.5, -2.0, -3.0, -4.0, -6.0])


def pack_weight(w, fmt):
    k, n = w.shape
    w = f64(np.asarray(w, np.float32).astype(ml_dtypes.bfloat16)).reshape(k // 32, 32, n)
    amax = np.abs(w).max(1)
    if fmt == "e4m3":
        byte = np.frexp(amax)[1] - 1 + 127 - 7
    else:
        mant, ex = np.frexp(amax / 6.0)
        byte = np.where(mant > 0.5, ex, ex - 1) + 127
    byte = np.clip(np.where(amax > 0, byte, 1), 1, 254)
    scaled = (w * np.exp2(127.0 - byte)[:, None, :]).reshape(k, n).astype(np.float32)
    by_word = np.ascontiguousarray(scaled.reshape(k // 512, 128, 4, n).transpose(0, 1, 3, 2))
    if fmt == "e4m3":
        words = by_word.astype(ml_dtypes.float8_e4m3fn).view(np.uint8)
    else:
        c = by_word.astype(ml_dtypes.float4_e2m1fn).view(np.uint8) & 0xF
        words = (c[..., 0::2] | (c[..., 1::2] << 4)).reshape(k // 512, 128, 2 * n)
    return np.ascontiguousarray(words), np.ascontiguousarray(byte.astype(np.uint8).reshape(k // 512, 16, n))


def unpack_weight(words, scales, fmt):
    g, _, n = scales.shape
    words = np.ascontiguousarray(words).reshape(g, 128, n, -1)
    if fmt == "e4m3":
        vals = words.view(ml_dtypes.float8_e4m3fn).astype(np.float64)
    else:
        nib = np.empty((g, 128, n, 4), np.uint8)
        nib[..., 0::2] = words & 0xF
        nib[..., 1::2] = words >> 4
        vals = E2M1[nib]
    vals = vals * np.repeat(np.exp2(scales.astype(np.float64) - 127.0), 8, axis=1)[..., None]
    return vals.transpose(0, 1, 3, 2).reshape(g * 512, n)


def gelu(v):
    return 0.5 * v * (1.0 + np.tanh(np.sqrt(2.0 / np.pi) * (v + 0.044715 * v**3)))


def bf(x):
    return np.asarray(x, np.float32).astype(ml_dtypes.bfloat16)


def planes(Y):
    n, m = Y.shape
    b = f64(bf(Y)).reshape(n // 32, 32, m)
    amax = np.abs(b).max(1)
    byte = np.clip(np.where(amax > 0, np.frexp(amax)[1] - 1 + 127 - 7, 1), 1, 254)
    codes = (b * np.exp2(127.0 - byte)[:, None, :]).reshape(n, m).astype(np.float32).astype(ml_dtypes.float8_e4m3fn).view(np.uint8)
    words = codes.reshape(n // 512, 128, 4, m).transpose(0, 1, 3, 2)
    return np.ascontiguousarray(words), np.ascontiguousarray(byte.astype(np.uint8).reshape(n // 512, 16, m))


K, H, N, T, S, P = 1536, 1024, 512, 2048, 512, 256

def setup_inputs():
    n = np.random.standard_normal
    s = mx_kscale(K)[:, None]
    u = mx_kscale(H)[:, None]
    tab_words, tab_scales = pack_weight(n((K, T)) * s, "e4m3")
    w1 = (0.54 * n((K, H)) / np.sqrt(K) / s).astype(np.float32)
    gh = (np.random.uniform(0.5, 2.0, H) * u[:, 0]).astype(np.float32)
    wa = (0.95 * n((H, N)) / np.sqrt(H) / u).astype(np.float32)
    wb_words, wb_scales = pack_weight(0.55 * n((K, N)) / np.sqrt(K) / s, "e2m1")
    wc_words, wc_scales = pack_weight(1.3 * n((H, N)) / np.sqrt(H) / u, "e4m3")
    sc = np.random.uniform(0.6, 3.0, N).astype(np.float32)
    th = n(N).astype(np.float32)
    sg = (np.random.choice([-1.0, 1.0], N) * np.random.uniform(0.8, 2.0, N)).astype(np.float32)
    gy = np.exp(0.8 * n(N)).astype(np.float32)
    return {"tab_words": tab_words, "tab_scales": tab_scales,
            "offs": striped(np.random.permutation(T)[:S]),
            "pos1": striped(np.random.permutation(S)[:P]),
            "pos2": striped(np.random.permutation(S)[:P]),
            "w1": w1, "gh": gh, "wa": wa,
            "wb_words": wb_words, "wb_scales": wb_scales,
            "wc_words": wc_words, "wc_scales": wc_scales,
            "sc": sc, "th": th, "sg": sg, "gy": gy}

def reference(tab_words, tab_scales, offs, pos1, pos2, w1, gh, wa, wb_words, wb_scales,
              wc_words, wc_scales, sc, th, sg, gy):
    v = unpack_weight(tab_words, tab_scales, "e4m3")[:, unstriped(offs)]
    wb = unpack_weight(wb_words, wb_scales, "e2m1")
    wc = unpack_weight(wc_words, wc_scales, "e4m3")
    h = np.sin(mxq(f64(w1), 0, "e4m3").T @ v) * f64(gh)[:, None]
    hq = mxq(h, 0, "e4m3")
    e = mxq(f64(wa), 0, "e4m3").T @ hq + wb.T @ v
    d = wc.T @ hq
    a = 1.0 / (1.0 + np.exp(-(f64(sc)[:, None] * e[:, unstriped(pos1)] + f64(th)[:, None])))
    c = d[:, unstriped(pos2)]
    y = np.abs(c - f64(sg)[:, None] * a) * f64(gy)[:, None]
    words, scales = planes(y)
    return y, words, scales

@@ -1,0 +1,306 @@
+import math
+from contextlib import ExitStack
+
+import concourse.mybir as mybir
+
+K, H, N, T, S, PICK = 1536, 1024, 512, 2048, 512, 256
+FLOPS = 2 * S * (K * H + H * N + K * N + H * N)
+
+F32 = mybir.dt.float32
+BF16 = mybir.dt.bfloat16
+I32 = mybir.dt.int32
+U32 = mybir.dt.uint32
+U16 = mybir.dt.uint16
+U8 = mybir.dt.uint8
+FP8X4 = mybir.dt.float8_e4m3fn_x4
+FP4X4 = mybir.dt.float4_e2m1fn_x4
+ACT = mybir.ActivationFunctionType
+ALU = mybir.AluOpType
+
+P = 128
+PACK = 4
+PASS = P * PACK
+KP = K // PASS
+HP = H // PASS
+CHUNK = 128
+CHUNKS = S // CHUNK
+QUADS = 4
+HALF = S // 2
+
+
+def tile_list_condenser_tube_watch_kernel(
+    tc, tab_words, tab_scales, offs, pos1, pos2, w1, gh, wa, wb_words, wb_scales,
+    wc_words, wc_scales, sc, th, sg, gy, out_0, out_1, out_2,
+):
+    nc = tc.nc
+    with ExitStack() as ctx:
+        keep = ctx.enter_context(tc.tile_pool(name="keep", bufs=1))
+        ring = ctx.enter_context(tc.tile_pool(name="ring", bufs=3))
+        psum = ctx.enter_context(tc.psum_pool(name="psum", bufs=1))
+
+        def held(shape, dtype, name):
+            return keep.tile(shape, dtype, name=name, align_bytes=64)
+
+        offs_sb = keep.tile([P, S // 16], U16, name="offs_sb")
+        pos1_sb = keep.tile([P, PICK // 16], U16, name="pos1_sb")
+        pos2_sb = keep.tile([P, PICK // 16], U16, name="pos2_sb")
+
+        tab_plane = held([P, KP * T], U8, "tab_plane")
+        wb_plane_raw = held([P, KP * N], U8, "wb_plane_raw")
+        wc_plane_raw = held([P, HP * N], U8, "wc_plane_raw")
+        nc.vector.memset(tab_plane[:].bitcast(I32), 0)
+        nc.gpsimd.memset(wb_plane_raw[:].bitcast(I32), 0)
+        nc.gpsimd.memset(wc_plane_raw[:].bitcast(I32), 0)
+        one = held([P, 1], F32, "one")
+        nc.vector.memset(one[:], 1.0)
+        phase = held([P, 1], F32, "phase")
+        nc.vector.tensor_scalar(phase[:], one[:], -math.pi / 8, None, ALU.mult)
+
+        def load_plane(queue, plane, scales, passes):
+            for q in range(QUADS):
+                queue.dma_start(
+                    plane[32 * q : 32 * q + 4, :].bitcast(I32).rearrange("r (a c) -> r a c", a=passes),
+                    scales[:, 4 * q : 4 * q + 4, :].rearrange("a r c -> r a c").bitcast(I32),
+                )
+
+        def load_rows(vec, name):
+            blocks = vec.shape[0] // PASS
+            rows = held([P, blocks, PACK], F32, name)
+            nc.sync.dma_start(rows[:], vec.rearrange("(b p t) -> p b t", p=P, t=PACK))
+            return rows
+
+
+        def load_weight(w, a, b, name):
+            raw = held([P, PACK, PASS], F32, name)
+            nc.sync.dma_start(
+                raw[:],
+                w[a * PASS : (a + 1) * PASS, b * PASS : (b + 1) * PASS].rearrange("(p j) c -> p j c", j=PACK),
+            )
+            return raw
+
+        def load_words(a):
+            words = held([P, T], I32, f"tab_sb{a}")
+            nc.sync.dma_start(words[:], tab_words[a].rearrange("p t i -> p (t i)").bitcast(I32))
+            return words
+
+        nc.sync.dma_start(offs_sb[:], offs)
+        tab_sb = [load_words(0)]
+        load_plane(nc.sync, tab_plane, tab_scales, KP)
+        w1_raw = {(0, 0): load_weight(w1, 0, 0, "w1_raw00")}
+        w1_raw[1, 0] = load_weight(w1, 1, 0, "w1_raw10")
+        gh_sb = load_rows(gh, "gh_sb")
+        load_plane(nc.sync, wb_plane_raw, wb_scales, KP)
+        tab_sb.append(load_words(1))
+        load_plane(nc.sync, wc_plane_raw, wc_scales, HP)
+        w1_raw[2, 0] = load_weight(w1, 2, 0, "w1_raw20")
+        nc.sync.dma_start(pos1_sb[:], pos1)
+        nc.sync.dma_start(pos2_sb[:], pos2)
+        sc_sb = load_rows(sc, "sc_sb")
+        th_sb = load_rows(th, "th_sb")
+        tab_sb.append(load_words(2))
+        sg_sb = load_rows(sg, "sg_sb")
+        gy_sb = load_rows(gy, "gy_sb")
+        for a in range(KP):
+            w1_raw[a, 1] = load_weight(w1, a, 1, f"w1_raw{a}1")
+        wb_raw = held([P, KP, N // 2], I32, "wb_raw")
+        nc.sync.dma_start(wb_raw[:], wb_words.rearrange("a p y -> p a y").bitcast(I32))
+        wa_raw = [load_weight(wa, 0, 0, "wa_raw0")]
+        wc_raw = held([P, HP, N], I32, "wc_raw")
+        nc.sync.dma_start(wc_raw[:], wc_words.rearrange("a p y i -> p a (y i)").bitcast(I32))
+        wa_raw.append(load_weight(wa, 1, 0, "wa_raw1"))
+
+        gain2 = held([P, HP, PACK], F32, "gain2")
+        nc.vector.tensor_scalar(gain2[:], gh_sb[:], 2.0, None, ALU.mult)
+
+        def quantise_weight(raw, copy, name):
+            dealt = ring.tile([P, PACK * PASS], BF16, name="dealt", align_bytes=64)
+            copy(
+                dealt[:].rearrange("p (t m j) -> p m j t", t=PACK, j=PACK),
+                raw[:].rearrange("p j (m t) -> p m j t", t=PACK),
+            )
+            codes = held([P, PASS], U32, name + "_codes")
+            plane = held([P, PASS], U8, name + "_plane")
+            nc.vector.quantize_mx(out=codes[:].bitcast(FP8X4), scales=plane[:], in_=dealt[:])
+            return codes, plane
+
+        def deal(raw, passes, dtype, name):
+            dealt = held([P, passes, N], dtype, name)
+            for a in range(0, passes, 2):
+                pair = slice(a, min(a + 2, passes))
+                nc.vector.tensor_copy(
+                    dealt[:, pair, :].rearrange("p a (t m) -> p a m t", t=PACK),
+                    raw[:, pair, :].rearrange("p a (m t) -> p a m t", t=PACK),
+                )
+            return dealt
+
+        def slot(t):
+            return slice(P * t, P * (t + 1))
+
+        v_plane = held([P, KP, S], U8, "v_plane")
+        for a in range(KP):
+            nc.vector.tensor_copy(v_plane[:, a, :], tab_plane[:, a * T : (a + 1) * T].indirect(offs_sb[:]))
+        v_codes = []
+
+        def first_stage_pass(banks, a, codes, plane):
+            for c in range(CHUNKS):
+                cols = slice(c * CHUNK, (c + 1) * CHUNK)
+                for t in range(PACK):
+                    nc.tensor.matmul_mx(
+                        out=banks[c][:, t, :],
+                        lhsT=codes[:, slot(t)].bitcast(FP8X4),
+                        lhsT_scale=plane[:, slot(t)],
+                        rhs=v_codes[a][:, cols].bitcast(FP8X4),
+                        rhs_scale=v_plane[:, a, cols],
+                        start=(a == 0 and t == 0),
+                        stop=(a == KP - 1 and t == PACK - 1),
+                    )
+
+        def shared_banks(shape, name):
+            return [psum.tile(shape, F32, name=f"{name}{c}", tag=f"shared{c}") for c in range(CHUNKS)]
+
+        banks = shared_banks([P, PACK, CHUNK], "x0_")
+        for a in range(KP):
+            codes, plane = quantise_weight(w1_raw[a, 0], nc.scalar.copy, f"w1_{a}0")
+            picked = held([P, S], U32, f"v_codes{a}")
+            pieces = CHUNKS if a == KP - 1 else 1
+            for c in range(pieces):
+                width = S // pieces
+                nc.vector.tensor_copy(
+                    picked[:, c * width : (c + 1) * width],
+                    tab_sb[a][:].bitcast(U32).indirect(offs_sb[:, c * width // 16 : (c + 1) * width // 16]),
+                )
+            v_codes.append(picked)
+            first_stage_pass(banks, a, codes, plane)
+
+        h_codes = [held([P, S], U32, f"h_codes{b}") for b in range(HP)]
+        h_plane = [held([P, S], U8, f"h_plane{b}") for b in range(HP)]
+
+        def quarter_sine(bank):
+            u = ring.tile([P, CHUNK, PACK], F32, name="u", bufs=CHUNKS)
+            nc.scalar.activation(u[:], bank[:].rearrange("p t n -> p n t"), ACT.Sin, bias=phase[:], scale=0.25)
+            return u
+
+        def finish_features(u, b, c):
+            cols = slice(c * CHUNK, (c + 1) * CHUNK)
+            u2 = ring.tile([P, CHUNK, PACK], F32, name="u2")
+            nc.scalar.activation(u2[:], u[:], ACT.Square)
+            c2 = ring.tile([P, CHUNK, PACK], F32, name="c2")
+            nc.scalar.activation(c2[:], u2[:], ACT.Square, bias=one[:], scale=-2.0)
+            h = ring.tile([P, CHUNK, PACK], BF16, name="h", align_bytes=64)
+            nc.vector.scalar_tensor_tensor(
+                h[:], c2[:], -0.5, gain2[:, b, :].unsqueeze(1).to_broadcast([P, CHUNK, PACK]), ALU.add, ALU.mult
+            )
+            nc.vector.quantize_mx(
+                out=h_codes[b][:, cols].bitcast(FP8X4),
+                scales=h_plane[b][:, cols],
+                in_=h[:].rearrange("p n t -> p (n t)"),
+            )
+
+        sines = [quarter_sine(banks[c]) for c in range(CHUNKS)]
+        banks = shared_banks([P, PACK, CHUNK], "x1_")
+        for a in range(KP):
+            codes, plane = quantise_weight(w1_raw[a, 1], nc.vector.tensor_copy, f"w1_{a}1")
+            first_stage_pass(banks, a, codes, plane)
+        for c in range(CHUNKS):
+            finish_features(sines[c], 0, c)
+        for c in range(CHUNKS):
+            finish_features(quarter_sine(banks[c]), 1, c)
+
+        wb_plane = deal(wb_plane_raw[:].rearrange("p (a y) -> p a y", a=KP), KP, U8, "wb_plane")
+        wc_plane = deal(wc_plane_raw[:].rearrange("p (a y) -> p a y", a=HP), HP, U8, "wc_plane")
+        wb_codes = deal(wb_raw[:].bitcast(U16), KP, U16, "wb_codes")
+        wa_q = [quantise_weight(wa_raw[0], nc.vector.tensor_copy, "wa_0")]
+        wc_codes = deal(wc_raw[:], HP, I32, "wc_codes")
+        wa_q.append(quantise_weight(wa_raw[1], nc.vector.tensor_copy, "wa_1"))
+
+        e_banks = [psum.tile([P, 2, HALF], F32, name=f"e_bank{i}", tag=f"e{i}") for i in range(CHUNKS)]
+        d_banks = shared_banks([P, 2, HALF], "d_bank")
+
+        def feature_pass(banks, codes, plane, b, t, first, width, start, stop):
+            half, at = divmod(first, HALF)
+            cols = slice(first, first + width)
+            nc.tensor.matmul_mx(
+                out=banks[2 * half + t // 2][:, t % 2, at : at + width],
+                lhsT=codes[:, slot(t)].bitcast(FP8X4),
+                lhsT_scale=plane[:, slot(t)],
+                rhs=h_codes[b][:, cols].bitcast(FP8X4),
+                rhs_scale=h_plane[b][:, cols],
+                start=start,
+                stop=stop,
+            )
+
+        for half in range(2):
+            cols = slice(half * HALF, (half + 1) * HALF)
+            for a in range(KP):
+                for t in range(PACK):
+                    nc.tensor.matmul_mx(
+                        out=e_banks[2 * half + t // 2][:, t % 2, :],
+                        lhsT=wb_codes[:, a, slot(t)].bitcast(FP4X4),
+                        lhsT_scale=wb_plane[:, a, slot(t)],
+                        rhs=v_codes[a][:, cols].bitcast(FP8X4),
+                        rhs_scale=v_plane[:, a, cols],
+                        start=(a == 0 and t % 2 == 0),
+                        stop=False,
+                    )
+        for half in range(2):
+            for t in range(PACK):
+                feature_pass(e_banks, wa_q[0][0], wa_q[0][1], 0, t, half * HALF, HALF, False, False)
+        for half in range(2):
+            for t in range(PACK):
+                feature_pass(d_banks, wc_codes[:, 0, :], wc_plane[:, 0, :], 0, t, half * HALF, HALF, t % 2 == 0, False)
+
+        e_sb = [held([P, S], F32, f"e{t}") for t in range(PACK)]
+        d_sb = held([P, PACK, S], F32, "d_sb")
+        for half in range(2):
+            cols = slice(half * HALF, (half + 1) * HALF)
+            for c in (2 * half, 2 * half + 1):
+                for t in range(PACK):
+                    feature_pass(e_banks, wa_q[1][0], wa_q[1][1], 1, t, c * CHUNK, CHUNK, False, c % 2 == 1 and t % 2 == 1)
+            for t in range(PACK):
+                feature_pass(d_banks, wc_codes[:, 1, :], wc_plane[:, 1, :], 1, t, half * HALF, HALF, False, t % 2 == 1)
+            for t in range(PACK):
+                copy = nc.scalar.copy if half == 0 else nc.vector.tensor_copy
+                copy(e_sb[t][:, cols], e_banks[2 * half + t // 2][:, t % 2, :])
+            for pair in range(2):
+                copy = nc.vector.tensor_copy if half == 1 and pair == 0 else nc.scalar.copy
+                copy(d_sb[:, 2 * pair : 2 * pair + 2, cols], d_banks[2 * half + pair][:])
+
+        y = held([P, PACK, PICK], F32, "y")
+        out_rows = out_0.rearrange("(p t) m -> p t m", t=PACK)
+        for t in range(PACK):
+            look = ring.tile([P, PICK], F32, name="look", bufs=PACK)
+            nc.scalar.activation(
+                look[:], e_sb[t][:].indirect(pos1_sb[:]), ACT.Sigmoid,
+                bias=th_sb[:, 0, t : t + 1], scale=sc_sb[:, 0, t : t + 1],
+            )
+            clean = ring.tile([P, PICK], F32, name="clean", bufs=PACK)
+            nc.vector.tensor_copy(clean[:], d_sb[:, t, :].indirect(pos2_sb[:]))
+            dev = ring.tile([P, PICK], F32, name="dev", bufs=PACK)
+            nc.vector.scalar_tensor_tensor(
+                dev[:], look[:], sg_sb[:, 0, t : t + 1], clean[:], ALU.mult, ALU.subtract
+            )
+            size = ring.tile([P, PICK], F32, name="size", bufs=PACK)
+            if t < PACK - 1:
+                nc.scalar.activation(size[:], dev[:], ACT.Abs)
+                nc.scalar.activation(y[:, t, :], size[:], ACT.Copy, scale=gy_sb[:, 0, t : t + 1])
+            else:
+                nc.vector.scalar_tensor_tensor(size[:], dev[:], -1.0, dev[:], ALU.mult, ALU.max)
+                nc.vector.tensor_scalar(y[:, t, :], size[:], gy_sb[:, 0, t : t + 1], None, ALU.mult)
+            nc.sync.dma_start(out_rows[:, t, :], y[:, t, :])
+
+        y_bf = held([P, PICK, PACK], BF16, "y_bf")
+        nc.vector.tensor_copy(
+            y_bf[:].rearrange("p (c i) t -> p c t i", i=4),
+            y[:].rearrange("p t (c i) -> p c t i", i=4),
+        )
+        y_codes = held([P, PICK], U32, "y_codes")
+        y_plane = held([P, PICK], U8, "y_plane")
+        nc.vector.quantize_mx(
+            out=y_codes[:].bitcast(FP8X4), scales=y_plane[:], in_=y_bf[:].rearrange("p m t -> p (m t)")
+        )
+        nc.sync.dma_start(out_1[0].rearrange("p m t -> p (m t)").bitcast(I32), y_codes[:].bitcast(I32))
+        for q in range(QUADS):
+            queue = nc.sync if q % 2 == 0 else nc.scalar
+            queue.dma_start(
+                out_2[0, 4 * q : 4 * q + 4, :].bitcast(I32), y_plane[32 * q : 32 * q + 4, :].bitcast(I32)
+            )

@@ -45,30 +45,39 @@ def tile_list_condenser_tube_watch_kernel(
         pos1_sb = keep.tile([P, PICK // 16], U16, name="pos1_sb")
         pos2_sb = keep.tile([P, PICK // 16], U16, name="pos2_sb")
 
-        tab_plane = held([P, KP * T], U8, "tab_plane")
-        wb_plane_raw = held([P, KP * N], U8, "wb_plane_raw")
-        wc_plane_raw = held([P, HP * N], U8, "wc_plane_raw")
-        nc.vector.memset(tab_plane[:].bitcast(I32), 0)
-        nc.gpsimd.memset(wb_plane_raw[:].bitcast(I32), 0)
-        nc.gpsimd.memset(wc_plane_raw[:].bitcast(I32), 0)
+        tab_plane = held([P, T], U8, "tab_plane")
+        wb_plane_raw = held([P, KP, N], U8, "wb_plane_raw")
+        wc_plane_raw = held([P, N], U8, "wc_plane_raw")
+        v_plane_low = held([P, KP, S], U8, "v_plane_low")
+        nc.gpsimd.memset(tab_plane[:].bitcast(I32), 0)
+        nc.vector.memset(wb_plane_raw[:].bitcast(I32), 0)
+        nc.vector.memset(wc_plane_raw[:].bitcast(I32), 0)
+        nc.vector.memset(v_plane_low[:].bitcast(I32), 0)
         one = held([P, 1], F32, "one")
         nc.vector.memset(one[:], 1.0)
         phase = held([P, 1], F32, "phase")
         nc.vector.tensor_scalar(phase[:], one[:], -math.pi / 8, None, ALU.mult)
 
-        def load_plane(queue, plane, scales, passes):
+        def load_packed_planes(queue, plane, scales, first):
+            passes = scales.shape[0]
             for q in range(QUADS):
-                queue.dma_start(
-                    plane[32 * q : 32 * q + 4, :].bitcast(I32).rearrange("r (a c) -> r a c", a=passes),
-                    scales[:, 4 * q : 4 * q + 4, :].rearrange("a r c -> r a c").bitcast(I32),
-                )
+                rows = slice(32 * q + first, 32 * q + first + 4 * passes)
+                queue.dma_start(plane[rows, :].bitcast(I32), scales[:, 4 * q : 4 * q + 4, :].bitcast(I32))
 
-        def load_rows(vec, name):
+        def load_rows(queue, vec, name):
             blocks = vec.shape[0] // PASS
             rows = held([P, blocks, PACK], F32, name)
-            nc.sync.dma_start(rows[:], vec.rearrange("(b p t) -> p b t", p=P, t=PACK))
+            queue.dma_start(rows[:], vec.rearrange("(b p t) -> p b t", p=P, t=PACK))
             return rows
 
+        load_packed_planes(nc.gpsimd, tab_plane, tab_scales, 4)
+        for r in range(4):
+            nc.scalar.dma_start(
+                wb_plane_raw[r:P:32, :, :].bitcast(I32),
+                wb_scales[:, r:16:4, :].rearrange("a q c -> q a c").bitcast(I32),
+            )
+        load_packed_planes(nc.scalar, wc_plane_raw, wc_scales, 0)
+        gh_sb = load_rows(nc.scalar, gh, "gh_sb")
 
         def load_weight(w, a, b, name):
             raw = held([P, PACK, PASS], F32, name)
@@ -85,29 +94,30 @@ def tile_list_condenser_tube_watch_kernel(
 
         nc.sync.dma_start(offs_sb[:], offs)
         tab_sb = [load_words(0)]
-        load_plane(nc.sync, tab_plane, tab_scales, KP)
         w1_raw = {(0, 0): load_weight(w1, 0, 0, "w1_raw00")}
         w1_raw[1, 0] = load_weight(w1, 1, 0, "w1_raw10")
-        gh_sb = load_rows(gh, "gh_sb")
-        load_plane(nc.sync, wb_plane_raw, wb_scales, KP)
         tab_sb.append(load_words(1))
-        load_plane(nc.sync, wc_plane_raw, wc_scales, HP)
         w1_raw[2, 0] = load_weight(w1, 2, 0, "w1_raw20")
-        nc.sync.dma_start(pos1_sb[:], pos1)
-        nc.sync.dma_start(pos2_sb[:], pos2)
-        sc_sb = load_rows(sc, "sc_sb")
-        th_sb = load_rows(th, "th_sb")
         tab_sb.append(load_words(2))
-        sg_sb = load_rows(sg, "sg_sb")
-        gy_sb = load_rows(gy, "gy_sb")
         for a in range(KP):
             w1_raw[a, 1] = load_weight(w1, a, 1, f"w1_raw{a}1")
+        v_plane = held([P, S], U8, "v_plane")
+        nc.vector.tensor_copy(v_plane[:], tab_plane[:].indirect(offs_sb[:]))
+        for a in range(KP):
+            lift = 4 * (a + 1)
+            nc.sync.dma_start(v_plane_low[0:100, a, :].bitcast(I32), v_plane[lift : lift + 100, :].bitcast(I32))
         wb_raw = held([P, KP, N // 2], I32, "wb_raw")
         nc.sync.dma_start(wb_raw[:], wb_words.rearrange("a p y -> p a y").bitcast(I32))
         wa_raw = [load_weight(wa, 0, 0, "wa_raw0")]
         wc_raw = held([P, HP, N], I32, "wc_raw")
         nc.sync.dma_start(wc_raw[:], wc_words.rearrange("a p y i -> p a (y i)").bitcast(I32))
         wa_raw.append(load_weight(wa, 1, 0, "wa_raw1"))
+        nc.sync.dma_start(pos1_sb[:], pos1)
+        nc.sync.dma_start(pos2_sb[:], pos2)
+        sc_sb = load_rows(nc.sync, sc, "sc_sb")
+        th_sb = load_rows(nc.sync, th, "th_sb")
+        sg_sb = load_rows(nc.sync, sg, "sg_sb")
+        gy_sb = load_rows(nc.sync, gy, "gy_sb")
 
         gain2 = held([P, HP, PACK], F32, "gain2")
         nc.vector.tensor_scalar(gain2[:], gh_sb[:], 2.0, None, ALU.mult)
@@ -123,22 +133,20 @@ def tile_list_condenser_tube_watch_kernel(
             nc.vector.quantize_mx(out=codes[:].bitcast(FP8X4), scales=plane[:], in_=dealt[:])
             return codes, plane
 
-        def deal(raw, passes, dtype, name):
+        def deal(raw, walk, dtype, name):
+            passes = raw.shape[1]
             dealt = held([P, passes, N], dtype, name)
             for a in range(0, passes, 2):
                 pair = slice(a, min(a + 2, passes))
                 nc.vector.tensor_copy(
-                    dealt[:, pair, :].rearrange("p a (t m) -> p a m t", t=PACK),
-                    raw[:, pair, :].rearrange("p a (m t) -> p a m t", t=PACK),
+                    dealt[:, pair, :].rearrange("p a (t m) -> " + walk, t=PACK),
+                    raw[:, pair, :].rearrange("p a (m t) -> " + walk, t=PACK),
                 )
             return dealt
 
         def slot(t):
             return slice(P * t, P * (t + 1))
 
-        v_plane = held([P, KP, S], U8, "v_plane")
-        for a in range(KP):
-            nc.vector.tensor_copy(v_plane[:, a, :], tab_plane[:, a * T : (a + 1) * T].indirect(offs_sb[:]))
         v_codes = []
 
         def first_stage_pass(banks, a, codes, plane):
@@ -150,7 +158,7 @@ def tile_list_condenser_tube_watch_kernel(
                         lhsT=codes[:, slot(t)].bitcast(FP8X4),
                         lhsT_scale=plane[:, slot(t)],
                         rhs=v_codes[a][:, cols].bitcast(FP8X4),
-                        rhs_scale=v_plane[:, a, cols],
+                        rhs_scale=v_plane[4 * (a + 1) : P, cols],
                         start=(a == 0 and t == 0),
                         stop=(a == KP - 1 and t == PACK - 1),
                     )
@@ -206,11 +214,11 @@ def tile_list_condenser_tube_watch_kernel(
         for c in range(CHUNKS):
             finish_features(quarter_sine(banks[c]), 1, c)
 
-        wb_plane = deal(wb_plane_raw[:].rearrange("p (a y) -> p a y", a=KP), KP, U8, "wb_plane")
-        wc_plane = deal(wc_plane_raw[:].rearrange("p (a y) -> p a y", a=HP), HP, U8, "wc_plane")
-        wb_codes = deal(wb_raw[:].bitcast(U16), KP, U16, "wb_codes")
+        wb_plane = deal(wb_plane_raw[:], "p a t m", U8, "wb_plane")
+        wc_plane = deal(wc_plane_raw[:].unsqueeze(1), "p a t m", U8, "wc_plane")
+        wb_codes = deal(wb_raw[:].bitcast(U16), "p a t m", U16, "wb_codes")
         wa_q = [quantise_weight(wa_raw[0], nc.vector.tensor_copy, "wa_0")]
-        wc_codes = deal(wc_raw[:], HP, I32, "wc_codes")
+        wc_codes = deal(wc_raw[:], "p a m t", I32, "wc_codes")
         wa_q.append(quantise_weight(wa_raw[1], nc.vector.tensor_copy, "wa_1"))
 
         e_banks = [psum.tile([P, 2, HALF], F32, name=f"e_bank{i}", tag=f"e{i}") for i in range(CHUNKS)]
@@ -238,7 +246,7 @@ def tile_list_condenser_tube_watch_kernel(
                         lhsT=wb_codes[:, a, slot(t)].bitcast(FP4X4),
                         lhsT_scale=wb_plane[:, a, slot(t)],
                         rhs=v_codes[a][:, cols].bitcast(FP8X4),
-                        rhs_scale=v_plane[:, a, cols],
+                        rhs_scale=v_plane_low[:, a, cols],
                         start=(a == 0 and t % 2 == 0),
                         stop=False,
                     )
@@ -247,7 +255,7 @@ def tile_list_condenser_tube_watch_kernel(
                 feature_pass(e_banks, wa_q[0][0], wa_q[0][1], 0, t, half * HALF, HALF, False, False)
         for half in range(2):
             for t in range(PACK):
-                feature_pass(d_banks, wc_codes[:, 0, :], wc_plane[:, 0, :], 0, t, half * HALF, HALF, t % 2 == 0, False)
+                feature_pass(d_banks, wc_codes[:, 0, :], wc_plane[0:P, 0, :], 0, t, half * HALF, HALF, t % 2 == 0, False)
 
         e_sb = [held([P, S], F32, f"e{t}") for t in range(PACK)]
         d_sb = held([P, PACK, S], F32, "d_sb")
@@ -257,7 +265,7 @@ def tile_list_condenser_tube_watch_kernel(
                 for t in range(PACK):
                     feature_pass(e_banks, wa_q[1][0], wa_q[1][1], 1, t, c * CHUNK, CHUNK, False, c % 2 == 1 and t % 2 == 1)
             for t in range(PACK):
-                feature_pass(d_banks, wc_codes[:, 1, :], wc_plane[:, 1, :], 1, t, half * HALF, HALF, False, t % 2 == 1)
+                feature_pass(d_banks, wc_codes[:, 1, :], wc_plane[4:P, 0, :], 1, t, half * HALF, HALF, False, t % 2 == 1)
             for t in range(PACK):
                 copy = nc.scalar.copy if half == 0 else nc.vector.tensor_copy
                 copy(e_sb[t][:, cols], e_banks[2 * half + t // 2][:, t % 2, :])

@@ -55,6 +55,8 @@ def tile_list_condenser_tube_watch_kernel(
         nc.vector.memset(v_plane_low[:].bitcast(I32), 0)
         one = held([P, 1], F32, "one")
         nc.vector.memset(one[:], 1.0)
+        warm = held([P, 1], F32, "warm")
+        nc.scalar.activation(warm[:], one[:], ACT.Sin)
         phase = held([P, 1], F32, "phase")
         nc.vector.tensor_scalar(phase[:], one[:], -math.pi / 8, None, ALU.mult)
 
@@ -194,6 +196,9 @@ def tile_list_condenser_tube_watch_kernel(
             nc.scalar.activation(u2[:], u[:], ACT.Square)
             c2 = ring.tile([P, CHUNK, PACK], F32, name="c2")
             nc.scalar.activation(c2[:], u2[:], ACT.Square, bias=one[:], scale=-2.0)
+            if b == HP - 1 and c == CHUNKS - 1:
+                warm_sigmoid = held([P, 1], F32, "warm_sigmoid")
+                nc.scalar.activation(warm_sigmoid[:], c2[:, 0, 0:1], ACT.Sigmoid)
             h = ring.tile([P, CHUNK, PACK], BF16, name="h", align_bytes=64)
             nc.vector.scalar_tensor_tensor(
                 h[:], c2[:], -0.5, gain2[:, b, :].unsqueeze(1).to_broadcast([P, CHUNK, PACK]), ALU.add, ALU.mult

import math
from contextlib import ExitStack

import concourse.mybir as mybir

K, H, N, T, S, PICK = 1536, 1024, 512, 2048, 512, 256
FLOPS = 2 * S * (K * H + H * N + K * N + H * N)

F32 = mybir.dt.float32
BF16 = mybir.dt.bfloat16
I32 = mybir.dt.int32
U32 = mybir.dt.uint32
U16 = mybir.dt.uint16
U8 = mybir.dt.uint8
FP8X4 = mybir.dt.float8_e4m3fn_x4
FP4X4 = mybir.dt.float4_e2m1fn_x4
ACT = mybir.ActivationFunctionType
ALU = mybir.AluOpType

P = 128
PACK = 4
PASS = P * PACK
KP = K // PASS
HP = H // PASS
CHUNK = 128
CHUNKS = S // CHUNK
QUADS = 4
HALF = S // 2


def tile_list_condenser_tube_watch_kernel(
    tc, tab_words, tab_scales, offs, pos1, pos2, w1, gh, wa, wb_words, wb_scales,
    wc_words, wc_scales, sc, th, sg, gy, out_0, out_1, out_2,
):
    nc = tc.nc
    with ExitStack() as ctx:
        keep = ctx.enter_context(tc.tile_pool(name="keep", bufs=1))
        ring = ctx.enter_context(tc.tile_pool(name="ring", bufs=3))
        psum = ctx.enter_context(tc.psum_pool(name="psum", bufs=1))

        def held(shape, dtype, name):
            return keep.tile(shape, dtype, name=name, align_bytes=64)

        offs_sb = keep.tile([P, S // 16], U16, name="offs_sb")
        pos1_sb = keep.tile([P, PICK // 16], U16, name="pos1_sb")
        pos2_sb = keep.tile([P, PICK // 16], U16, name="pos2_sb")

        tab_plane = held([P, T], U8, "tab_plane")
        wb_plane_raw = held([P, KP, N], U8, "wb_plane_raw")
        wc_plane_raw = held([P, N], U8, "wc_plane_raw")
        v_plane_low = held([P, KP, S], U8, "v_plane_low")
        nc.gpsimd.memset(tab_plane[:].bitcast(I32), 0)
        nc.vector.memset(wb_plane_raw[:].bitcast(I32), 0)
        nc.vector.memset(wc_plane_raw[:].bitcast(I32), 0)
        nc.vector.memset(v_plane_low[:].bitcast(I32), 0)
        one = held([P, 1], F32, "one")
        nc.vector.memset(one[:], 1.0)
        warm = held([P, 1], F32, "warm")
        nc.scalar.activation(warm[:], one[:], ACT.Sin)
        phase = held([P, 1], F32, "phase")
        nc.vector.tensor_scalar(phase[:], one[:], -math.pi / 8, None, ALU.mult)

        def load_packed_planes(queue, plane, scales, first):
            passes = scales.shape[0]
            for q in range(QUADS):
                rows = slice(32 * q + first, 32 * q + first + 4 * passes)
                queue.dma_start(plane[rows, :].bitcast(I32), scales[:, 4 * q : 4 * q + 4, :].bitcast(I32))

        def load_rows(queue, vec, name):
            blocks = vec.shape[0] // PASS
            rows = held([P, blocks, PACK], F32, name)
            queue.dma_start(rows[:], vec.rearrange("(b p t) -> p b t", p=P, t=PACK))
            return rows

        load_packed_planes(nc.gpsimd, tab_plane, tab_scales, 4)
        for r in range(4):
            nc.scalar.dma_start(
                wb_plane_raw[r:P:32, :, :].bitcast(I32),
                wb_scales[:, r:16:4, :].rearrange("a q c -> q a c").bitcast(I32),
            )
        load_packed_planes(nc.scalar, wc_plane_raw, wc_scales, 0)
        gh_sb = load_rows(nc.scalar, gh, "gh_sb")

        def load_weight(w, a, b, name):
            raw = held([P, PACK, PASS], F32, name)
            nc.sync.dma_start(
                raw[:],
                w[a * PASS : (a + 1) * PASS, b * PASS : (b + 1) * PASS].rearrange("(p j) c -> p j c", j=PACK),
            )
            return raw

        def load_words(a):
            words = held([P, T], I32, f"tab_sb{a}")
            nc.sync.dma_start(words[:], tab_words[a].rearrange("p t i -> p (t i)").bitcast(I32))
            return words

        nc.sync.dma_start(offs_sb[:], offs)
        tab_sb = [load_words(0)]
        w1_raw = {(0, 0): load_weight(w1, 0, 0, "w1_raw00")}
        w1_raw[1, 0] = load_weight(w1, 1, 0, "w1_raw10")
        tab_sb.append(load_words(1))
        w1_raw[2, 0] = load_weight(w1, 2, 0, "w1_raw20")
        tab_sb.append(load_words(2))
        for a in range(KP):
            w1_raw[a, 1] = load_weight(w1, a, 1, f"w1_raw{a}1")
        v_plane = held([P, S], U8, "v_plane")
        nc.vector.tensor_copy(v_plane[:], tab_plane[:].indirect(offs_sb[:]))
        for a in range(KP):
            lift = 4 * (a + 1)
            nc.sync.dma_start(v_plane_low[0:100, a, :].bitcast(I32), v_plane[lift : lift + 100, :].bitcast(I32))
        wb_raw = held([P, KP, N // 2], I32, "wb_raw")
        nc.sync.dma_start(wb_raw[:], wb_words.rearrange("a p y -> p a y").bitcast(I32))
        wa_raw = [load_weight(wa, 0, 0, "wa_raw0")]
        wc_raw = held([P, HP, N], I32, "wc_raw")
        nc.sync.dma_start(wc_raw[:], wc_words.rearrange("a p y i -> p a (y i)").bitcast(I32))
        wa_raw.append(load_weight(wa, 1, 0, "wa_raw1"))
        nc.sync.dma_start(pos1_sb[:], pos1)
        nc.sync.dma_start(pos2_sb[:], pos2)
        sc_sb = load_rows(nc.sync, sc, "sc_sb")
        th_sb = load_rows(nc.sync, th, "th_sb")
        sg_sb = load_rows(nc.sync, sg, "sg_sb")
        gy_sb = load_rows(nc.sync, gy, "gy_sb")

        gain2 = held([P, HP, PACK], F32, "gain2")
        nc.vector.tensor_scalar(gain2[:], gh_sb[:], 2.0, None, ALU.mult)

        def quantise_weight(raw, copy, name):
            dealt = ring.tile([P, PACK * PASS], BF16, name="dealt", align_bytes=64)
            copy(
                dealt[:].rearrange("p (t m j) -> p m j t", t=PACK, j=PACK),
                raw[:].rearrange("p j (m t) -> p m j t", t=PACK),
            )
            codes = held([P, PASS], U32, name + "_codes")
            plane = held([P, PASS], U8, name + "_plane")
            nc.vector.quantize_mx(out=codes[:].bitcast(FP8X4), scales=plane[:], in_=dealt[:])
            return codes, plane

        def deal(raw, walk, dtype, name):
            passes = raw.shape[1]
            dealt = held([P, passes, N], dtype, name)
            for a in range(0, passes, 2):
                pair = slice(a, min(a + 2, passes))
                nc.vector.tensor_copy(
                    dealt[:, pair, :].rearrange("p a (t m) -> " + walk, t=PACK),
                    raw[:, pair, :].rearrange("p a (m t) -> " + walk, t=PACK),
                )
            return dealt

        def slot(t):
            return slice(P * t, P * (t + 1))

        v_codes = []

        def first_stage_pass(banks, a, codes, plane):
            for c in range(CHUNKS):
                cols = slice(c * CHUNK, (c + 1) * CHUNK)
                for t in range(PACK):
                    nc.tensor.matmul_mx(
                        out=banks[c][:, t, :],
                        lhsT=codes[:, slot(t)].bitcast(FP8X4),
                        lhsT_scale=plane[:, slot(t)],
                        rhs=v_codes[a][:, cols].bitcast(FP8X4),
                        rhs_scale=v_plane[4 * (a + 1) : P, cols],
                        start=(a == 0 and t == 0),
                        stop=(a == KP - 1 and t == PACK - 1),
                    )

        def shared_banks(shape, name):
            return [psum.tile(shape, F32, name=f"{name}{c}", tag=f"shared{c}") for c in range(CHUNKS)]

        banks = shared_banks([P, PACK, CHUNK], "x0_")
        for a in range(KP):
            codes, plane = quantise_weight(w1_raw[a, 0], nc.scalar.copy, f"w1_{a}0")
            picked = held([P, S], U32, f"v_codes{a}")
            pieces = CHUNKS if a == KP - 1 else 1
            for c in range(pieces):
                width = S // pieces
                nc.vector.tensor_copy(
                    picked[:, c * width : (c + 1) * width],
                    tab_sb[a][:].bitcast(U32).indirect(offs_sb[:, c * width // 16 : (c + 1) * width // 16]),
                )
            v_codes.append(picked)
            first_stage_pass(banks, a, codes, plane)

        h_codes = [held([P, S], U32, f"h_codes{b}") for b in range(HP)]
        h_plane = [held([P, S], U8, f"h_plane{b}") for b in range(HP)]

        def quarter_sine(bank):
            u = ring.tile([P, CHUNK, PACK], F32, name="u", bufs=CHUNKS)
            nc.scalar.activation(u[:], bank[:].rearrange("p t n -> p n t"), ACT.Sin, bias=phase[:], scale=0.25)
            return u

        def finish_features(u, b, c):
            cols = slice(c * CHUNK, (c + 1) * CHUNK)
            u2 = ring.tile([P, CHUNK, PACK], F32, name="u2")
            nc.scalar.activation(u2[:], u[:], ACT.Square)
            c2 = ring.tile([P, CHUNK, PACK], F32, name="c2")
            nc.scalar.activation(c2[:], u2[:], ACT.Square, bias=one[:], scale=-2.0)
            if b == HP - 1 and c == CHUNKS - 1:
                warm_sigmoid = held([P, 1], F32, "warm_sigmoid")
                nc.scalar.activation(warm_sigmoid[:], c2[:, 0, 0:1], ACT.Sigmoid)
            h = ring.tile([P, CHUNK, PACK], BF16, name="h", align_bytes=64)
            nc.vector.scalar_tensor_tensor(
                h[:], c2[:], -0.5, gain2[:, b, :].unsqueeze(1).to_broadcast([P, CHUNK, PACK]), ALU.add, ALU.mult
            )
            nc.vector.quantize_mx(
                out=h_codes[b][:, cols].bitcast(FP8X4),
                scales=h_plane[b][:, cols],
                in_=h[:].rearrange("p n t -> p (n t)"),
            )

        sines = [quarter_sine(banks[c]) for c in range(CHUNKS)]
        banks = shared_banks([P, PACK, CHUNK], "x1_")
        for a in range(KP):
            codes, plane = quantise_weight(w1_raw[a, 1], nc.vector.tensor_copy, f"w1_{a}1")
            first_stage_pass(banks, a, codes, plane)
        for c in range(CHUNKS):
            finish_features(sines[c], 0, c)
        for c in range(CHUNKS):
            finish_features(quarter_sine(banks[c]), 1, c)

        wb_plane = deal(wb_plane_raw[:], "p a t m", U8, "wb_plane")
        wc_plane = deal(wc_plane_raw[:].unsqueeze(1), "p a t m", U8, "wc_plane")
        wb_codes = deal(wb_raw[:].bitcast(U16), "p a t m", U16, "wb_codes")
        wa_q = [quantise_weight(wa_raw[0], nc.vector.tensor_copy, "wa_0")]
        wc_codes = deal(wc_raw[:], "p a m t", I32, "wc_codes")
        wa_q.append(quantise_weight(wa_raw[1], nc.vector.tensor_copy, "wa_1"))

        e_banks = [psum.tile([P, 2, HALF], F32, name=f"e_bank{i}", tag=f"e{i}") for i in range(CHUNKS)]
        d_banks = shared_banks([P, 2, HALF], "d_bank")

        def feature_pass(banks, codes, plane, b, t, first, width, start, stop):
            half, at = divmod(first, HALF)
            cols = slice(first, first + width)
            nc.tensor.matmul_mx(
                out=banks[2 * half + t // 2][:, t % 2, at : at + width],
                lhsT=codes[:, slot(t)].bitcast(FP8X4),
                lhsT_scale=plane[:, slot(t)],
                rhs=h_codes[b][:, cols].bitcast(FP8X4),
                rhs_scale=h_plane[b][:, cols],
                start=start,
                stop=stop,
            )

        for half in range(2):
            cols = slice(half * HALF, (half + 1) * HALF)
            for a in range(KP):
                for t in range(PACK):
                    nc.tensor.matmul_mx(
                        out=e_banks[2 * half + t // 2][:, t % 2, :],
                        lhsT=wb_codes[:, a, slot(t)].bitcast(FP4X4),
                        lhsT_scale=wb_plane[:, a, slot(t)],
                        rhs=v_codes[a][:, cols].bitcast(FP8X4),
                        rhs_scale=v_plane_low[:, a, cols],
                        start=(a == 0 and t % 2 == 0),
                        stop=False,
                    )
        for half in range(2):
            for t in range(PACK):
                feature_pass(e_banks, wa_q[0][0], wa_q[0][1], 0, t, half * HALF, HALF, False, False)
        for half in range(2):
            for t in range(PACK):
                feature_pass(d_banks, wc_codes[:, 0, :], wc_plane[0:P, 0, :], 0, t, half * HALF, HALF, t % 2 == 0, False)

        e_sb = [held([P, S], F32, f"e{t}") for t in range(PACK)]
        d_sb = held([P, PACK, S], F32, "d_sb")
        for half in range(2):
            cols = slice(half * HALF, (half + 1) * HALF)
            for c in (2 * half, 2 * half + 1):
                for t in range(PACK):
                    feature_pass(e_banks, wa_q[1][0], wa_q[1][1], 1, t, c * CHUNK, CHUNK, False, c % 2 == 1 and t % 2 == 1)
            for t in range(PACK):
                feature_pass(d_banks, wc_codes[:, 1, :], wc_plane[4:P, 0, :], 1, t, half * HALF, HALF, False, t % 2 == 1)
            for t in range(PACK):
                copy = nc.scalar.copy if half == 0 else nc.vector.tensor_copy
                copy(e_sb[t][:, cols], e_banks[2 * half + t // 2][:, t % 2, :])
            for pair in range(2):
                copy = nc.vector.tensor_copy if half == 1 and pair == 0 else nc.scalar.copy
                copy(d_sb[:, 2 * pair : 2 * pair + 2, cols], d_banks[2 * half + pair][:])

        y = held([P, PACK, PICK], F32, "y")
        out_rows = out_0.rearrange("(p t) m -> p t m", t=PACK)
        for t in range(PACK):
            look = ring.tile([P, PICK], F32, name="look", bufs=PACK)
            nc.scalar.activation(
                look[:], e_sb[t][:].indirect(pos1_sb[:]), ACT.Sigmoid,
                bias=th_sb[:, 0, t : t + 1], scale=sc_sb[:, 0, t : t + 1],
            )
            clean = ring.tile([P, PICK], F32, name="clean", bufs=PACK)
            nc.vector.tensor_copy(clean[:], d_sb[:, t, :].indirect(pos2_sb[:]))
            dev = ring.tile([P, PICK], F32, name="dev", bufs=PACK)
            nc.vector.scalar_tensor_tensor(
                dev[:], look[:], sg_sb[:, 0, t : t + 1], clean[:], ALU.mult, ALU.subtract
            )
            size = ring.tile([P, PICK], F32, name="size", bufs=PACK)
            if t < PACK - 1:
                nc.scalar.activation(size[:], dev[:], ACT.Abs)
                nc.scalar.activation(y[:, t, :], size[:], ACT.Copy, scale=gy_sb[:, 0, t : t + 1])
            else:
                nc.vector.scalar_tensor_tensor(size[:], dev[:], -1.0, dev[:], ALU.mult, ALU.max)
                nc.vector.tensor_scalar(y[:, t, :], size[:], gy_sb[:, 0, t : t + 1], None, ALU.mult)
            nc.sync.dma_start(out_rows[:, t, :], y[:, t, :])

        y_bf = held([P, PICK, PACK], BF16, "y_bf")
        nc.vector.tensor_copy(
            y_bf[:].rearrange("p (c i) t -> p c t i", i=4),
            y[:].rearrange("p t (c i) -> p c t i", i=4),
        )
        y_codes = held([P, PICK], U32, "y_codes")
        y_plane = held([P, PICK], U8, "y_plane")
        nc.vector.quantize_mx(
            out=y_codes[:].bitcast(FP8X4), scales=y_plane[:], in_=y_bf[:].rearrange("p m t -> p (m t)")
        )
        nc.sync.dma_start(out_1[0].rearrange("p m t -> p (m t)").bitcast(I32), y_codes[:].bitcast(I32))
        for q in range(QUADS):
            queue = nc.sync if q % 2 == 0 else nc.scalar
            queue.dma_start(
                out_2[0, 4 * q : 4 * q + 4, :].bitcast(I32), y_plane[32 * q : 32 * q + 4, :].bitcast(I32)
            )
